import numpy as np
CORES = [50,106,114,52,108,116]
N = 6
KT, C = 1, 64
def setup_inputs(rng):
    return {"x": rng.standard_normal((N, 128, KT * C), dtype=np.float32)}
def setup_inputs_big(rng):
    d = setup_inputs(rng)
    for k in ("x",): d[k] = (d[k].astype(np.float32) * 1024.0).astype(d[k].dtype)
    return d
def setup_inputs_small(rng):
    d = setup_inputs(rng)
    for k in ("x",): d[k] = (d[k].astype(np.float32) * (1 / 1024.0)).astype(d[k].dtype)
    return d
def setup_inputs_apart(rng):
    d = setup_inputs(rng)
    f = (10.0 ** rng.permutation(np.linspace(-1.5, 1.5, N))).astype(np.float32).reshape(N, 1, 1)
    for k in ("x",): d[k] = (d[k].astype(np.float32) * f).astype(d[k].dtype)
    return d
def reference(x):
    X = x.astype(np.float64)
    y = np.full((N, C, N * C), np.nan)
    for r in range(N):
        for i in range(N):
            s = i
            if s != r: y[r][:, C * i:C * i + C] = sum(X[r][:, C * t:C * t + C].T @ X[s][:, C * t:C * t + C] for t in range(KT))
    return {"y": y.astype(np.float32 if x.dtype != np.float64 else np.float64)}

from concourse.bass import DstId, RemoteDMATransfer

NR, C = 6, 64

SCRATCH = {
    "xs": ("sbuf", [128, NR * C], "float32"),
    "o": ("sbuf", [128, NR * C], "float32"),
}
for _b in range(NR):
    SCRATCH["ps%d" % _b] = ("psum", [128, 512], "float32")

SEMAPHORES = (["ld", "loc", "st_sync", "st_scalar"]
              + ["arr%d" % _b for _b in range(NR)]
              + ["mm%d" % _b for _b in range(NR)]
              + ["cp%d" % _b for _b in range(NR)])


def _bits(mask):
    return [b for b in range(mask.bit_length()) if (mask >> b) & 1]


def _mask_of(bits):
    m = 0
    for b in bits:
        m |= 1 << b
    return m


def _plan(cores, topo):
    chips = []
    for c in cores:
        if topo.chip(c) not in chips:
            chips.append(topo.chip(c))
    on = {ch: [c for c in cores if topo.chip(c) == ch] for ch in chips}
    rank = {c: i for i, c in enumerate(cores)}

    serves = {c: [] for c in cores}
    for p in chips:
        others = [q for q in chips if q != p]
        able = {q: [c for c in on[p] if all(topo.may_write(c, d) for d in on[q])] for q in others}
        for q in sorted(others, key=lambda q: len(able[q])):
            gate = min(able[q], key=lambda c: len(serves[c]))
            serves[gate].append(q)

    first, late, passed = {c: [] for c in cores}, {c: [] for c in cores}, {c: [] for c in cores}
    when = {c: [] for c in cores}
    for c in cores:
        near = [d for d in on[topo.chip(c)] if d != c]
        busy = len(serves[c]) > 1
        own_near = [(rank[c], near)] if near else []
        for d in near:
            when[d].append((1.0, rank[c], c))
        own_far = []
        for q in serves[c]:
            if busy:
                head = ([d for d in on[q] if topo.die(d) == topo.die(c)] + on[q])[0]
                rest = [d for d in on[q] if d != head]
                own_far.append(head)
                when[head].append((2.0, rank[c], c))
                if rest:
                    passed[head].append((rank[c], rest))
                    for d in rest:
                        when[d].append((3.5, rank[c], head))
            else:
                own_far += on[q]
                for d in on[q]:
                    when[d].append((2.0, rank[c], c))
        own_far = [(rank[c], own_far)] if own_far else []
        first[c] = own_near + own_far if any(serves[d] for d in near) else own_far + own_near
        far = [d for q in serves[c] for d in on[q]]
        for n in near:
            if far:
                late[c].append((rank[n], far))
                for d in far:
                    when[d].append((4.0 if busy else 3.0, rank[n], c))
    sends = {c: first[c] + late[c] + passed[c] for c in cores}
    arrivals = {c: [(b, s) for _, b, s in sorted(when[c])] for c in cores}
    return sends, arrivals


def _engines(src, dst, cores, sends, topo):
    if topo.chip(src) != topo.chip(dst):
        return topo.mask(src, dst)
    whole = topo.mask(src, dst)
    leaves = any(topo.chip(d) != topo.chip(src) for _, ds in sends[src] for d in ds)
    if not leaves:
        return _mask_of(_bits(whole)[::2])
    far = [d for d in cores if topo.chip(d) != topo.chip(src)][0]
    return whole & ~topo.mask(src, far)


def rank_program(g, core, T, topo):
    r = T.rank_of(core)
    if r is None:
        return
    cores = list(T.cores)
    sends, arrivals = _plan(cores, topo)

    def blk(t, b):
        return t[:, b * C:(b + 1) * C]

    g.sync.dma_start(blk(T.xs, r), T.x[:, :]).then_inc(T.sem.ld, 16)

    g.wait_ge(T.sem.ld, 16)
    count_in = {b: len(_bits(_engines(s, core, cores, sends, topo))) for b, s in arrivals[core]}
    left = 0
    for b, dests in sends[core]:
        if b != r:
            g.wait_ge(T.sem["arr%d" % b], count_in[b])
        mask = _engines(core, dests[0], cores, sends, topo)
        ids = []
        for d in dests:
            rid, pid, _ = topo.addr(d)
            ids.append(DstId(rid=rid, pnc=pid))
        g.remote_dma_fused(
            [RemoteDMATransfer(dst_ids=ids, dma_engine_mask=mask, remote_sem=T.sem["arr%d" % b],
                               srcs=[blk(T.xs, b)], dsts=[blk(T.xs, b) for _ in dests], alu_op=0)],
            local_sem=T.sem.loc)
        left += len(_bits(mask))

    g.tensor.wait_ge(T.sem.ld, 16)
    stores = {"st_sync": 0, "st_scalar": 0}
    for i, (b, _) in enumerate(arrivals[core]):
        ps = T["ps%d" % b][0:C, 0:C]
        g.tensor.wait_ge(T.sem["arr%d" % b], count_in[b])
        g.tensor.matmul(ps, blk(T.xs, r), blk(T.xs, b), start=True, stop=True).then_inc(T.sem["mm%d" % b], 1)
        g.vector.wait_ge(T.sem["mm%d" % b], 1)
        g.vector.tensor_copy(T.o[0:C, b * C:(b + 1) * C], ps).then_inc(T.sem["cp%d" % b], 1)
        q, name = ((g.sync, "st_sync"), (g.scalar, "st_scalar"))[i % 2]
        q.wait_ge(T.sem["cp%d" % b], 1)
        q.dma_start(T.y[:, b * C:(b + 1) * C], T.o[0:C, b * C:(b + 1) * C]).then_inc(T.sem[name], 16)
        stores[name] += 16

    g.wait_ge(T.sem.loc, left)
    g.sync.wait_ge(T.sem.st_sync, stores["st_sync"])
    g.scalar.wait_ge(T.sem.st_scalar, stores["st_scalar"])
